import numpy as np, ml_dtypes
CORES = [19,147,275,403]
N = 4
import mx_ref
NC = 256
WID = [128,158,256,226]
BF = ml_dtypes.bfloat16
def setup_inputs(rng):
    def f(*shape):
        return mx_ref.flush((rng.standard_normal(shape, dtype=np.float32) * np.exp2(rng.integers(-2, 3, shape[:-1] + (1,)))).astype(BF))
    return {"w": f(N, 128, 512), "x": f(N, 128, 4 * NC)}
def setup_inputs_blocks(rng):
    d = setup_inputs(rng)
    for k in ("w", "x"): d[k] = mx_ref.spread(d[k], rng, 4)
    return d
def setup_inputs_wide(rng):
    d = setup_inputs(rng)
    for k in ("w", "x"): d[k] = mx_ref.flush((d[k].astype(np.float32) * np.exp2(rng.integers(-8, 9, (N, 1, 1))).astype(np.float32)).astype(BF))
    return d
def setup_inputs_zeros(rng):
    d = setup_inputs(rng); v = d["x"].reshape(N, 128, -1, 4).copy()
    v[np.broadcast_to((rng.random((N, 1, v.shape[2], 1)) < 0.33), v.shape)] = 0
    d["x"] = v.reshape(d["x"].shape)
    return d
def reference(w, x):
    OFF = [sum(WID[:j]) for j in range(N + 1)]
    y = np.zeros((N, 128, OFF[N]), np.float32)
    for r in range(N):
        qw = mx_ref.quantize(w[r])
        for j in range(N):
            y[r][:, OFF[j]:OFF[j + 1]] = mx_ref.matmul(qw, mx_ref.quantize(x[j][:, :4 * WID[j]]))
    return {"y": y}

@@ -1,0 +1,158 @@
+from concourse.bass import DstId, RemoteDMATransfer
+from concourse.mybir import dt, ActivationFunctionType
+
+N = 4
+SLOT = 256
+BANK = 512
+
+SCRATCH = {
+    "xb": ("sbuf", [128, 4 * SLOT], "bfloat16"),
+    "wb": ("sbuf", [128, 512], "bfloat16"),
+    "cw": ("sbuf", [128, 128], "float8_e4m3fn_x4"),
+    "sw": ("sbuf", [128, 128], "uint8"),
+    "cx": ("sbuf", [128, N * SLOT], "float8_e4m3fn_x4"),
+    "sx": ("sbuf", [128, N * SLOT], "uint8"),
+    "ps": ("psum", [128, N * BANK], "float32"),
+    "yb": ("sbuf", [128, N * SLOT], "float32"),
+}
+SEMAPHORES = (["xl", "wl", "qx", "qw", "sent", "st", "sf"]
+              + ["%s%d" % (p, j) for p in ("ca", "cb", "sc", "mm", "cp") for j in range(N)])
+
+
+def rank_program(g, core, T, topo):
+    r = T.rank_of(core)
+    if r is None:
+        return
+    cores, wid = T.cores, T.tables["WID"]
+    off = [sum(wid[:j]) for j in range(N + 1)]
+    S = T.sem
+
+    def near(j):
+        return [k for k in range(N) if k != j and topo.may_write(cores[j], cores[k])]
+
+    def far(j):
+        return [k for k in range(N) if k != j and k not in near(j)][0]
+
+    def by_switch(j):
+        return [k for k in near(j) if topo.same_plane(cores[j], cores[k])][0]
+
+    def by_cable(j):
+        return [k for k in near(j) if k != by_switch(j)][0]
+
+    def engines(a, b):
+        m = topo.mask(cores[a], cores[b])
+        return [1 << i for i in range(16) if (m >> i) & 1]
+
+    def own_mask(a, b):
+        e = engines(a, b)
+        return e[0::2] if b == by_switch(a) else e[1::2]
+
+    def dst_id(k):
+        rid, pid = topo.addr(cores[k], core)
+        return DstId(rid=rid, pnc=pid)
+
+    def cols(j, piece):
+        h = wid[j] // 2
+        a, b = {"a": (0, h), "b": (h, wid[j]), "all": (0, wid[j])}[piece]
+        return j * SLOT + a, j * SLOT + b
+
+    def codes(j, piece):
+        a, b = cols(j, piece)
+        return T.cx[:, a:b]
+
+    def plane(j, piece="all"):
+        a, b = cols(j, piece)
+        return T.sx[:, a:b]
+
+    def wire(j, what):
+        if what == "s":
+            return plane(j), S["sc%d" % j]
+        return codes(j, what).bitcast(dt.uint8), S["c%s%d" % (what, j)]
+
+    def landed(j, what):
+        if j in near(r):
+            return len(own_mask(j, r))
+        relay = by_cable(j) if what == "b" else by_switch(j)
+        return len(engines(relay, r))
+
+    nsw, ncb, nfar = by_switch(r), by_cable(r), far(r)
+    w_r = wid[r]
+
+    g.sync.dma_start(T.xb[:, :4 * w_r], T.x[:, :4 * w_r]).then_inc(S.xl, 16)
+    g.sync.dma_start(T.wb[:], T.w[:]).then_inc(S.wl, 16)
+
+    g.vector.wait_ge(S.xl, 16)
+    g.vector.quantize_mx(codes(r, "all"), plane(r), T.xb[:, :4 * w_r]).then_inc(S.qx, 1)
+    g.vector.wait_ge(S.wl, 16)
+    g.vector.quantize_mx(T.cw[:], T.sw[:], T.wb[:]).then_inc(S.qw, 1)
+
+    sent = [0]
+
+    def send_both(to_switch, to_cable):
+        trs = []
+        for k, what in ((nsw, to_switch), (ncb, to_cable)):
+            ap, sem = wire(r, what)
+            m = own_mask(r, k)
+            trs.append(RemoteDMATransfer(dst_ids=[dst_id(k)], dma_engine_mask=sum(m), remote_sem=sem, src=ap, dst=ap))
+            sent[0] += len(m)
+        g.remote_dma_fused(trs, local_sem=S.sent)
+
+    g.wait_ge(S.qx, 1)
+    send_both("a", "b")
+    send_both("s", "s")
+    send_both("b", "a")
+
+    def pass_on(j, what):
+        ap, sem = wire(j, what)
+        k = far(j)
+        m = engines(r, k)
+        rid, pid = topo.addr(cores[k], core)
+        g.wait_ge(sem, landed(j, what))
+        g.remote_dma(ap, ap, sem, S.sent, pid, rid, sum(m))
+        sent[0] += len(m)
+
+    order = sorted(near(r), key=lambda j: wid[j])
+    for j in order:
+        if r == by_switch(j):
+            pass_on(j, "a")
+            pass_on(j, "s")
+        else:
+            pass_on(j, "b")
+
+    g.tensor.wait_ge(S.qx, 1)
+    g.tensor.wait_ge(S.qw, 1)
+    for j in [r] + order + [nfar]:
+        if j != r:
+            for what in ("a", "b", "s"):
+                g.tensor.wait_ge(wire(j, what)[1], landed(j, what))
+        g.tensor.matmul_mx(T.ps[:, j * BANK:j * BANK + wid[j]], T.cw[:], T.sw[:], codes(j, "all"), plane(j),
+                           True, True).then_inc(S["mm%d" % j], 1)
+
+    def product(j):
+        return T.ps[:, j * BANK:j * BANK + wid[j]]
+
+    def staged(j):
+        return T.yb[:, j * SLOT:j * SLOT + wid[j]]
+
+    def y_block(j):
+        return T.y[:, off[j]:off[j + 1]]
+
+    for j in [r] + order:
+        g.vector.wait_ge(S["mm%d" % j], 1)
+        g.vector.tensor_copy(staged(j), product(j)).then_inc(S["cp%d" % j], 1)
+
+    g.sync.wait_ge(S["cp%d" % r], 1)
+    g.sync.wait_ge(S["cp%d" % order[0]], 1)
+    g.sync.dma_start(y_block(r), staged(r)).then_inc(S.st, 16)
+    g.sync.dma_start(y_block(order[0]), staged(order[0])).then_inc(S.st, 16)
+    g.sync.wait_ge(S["cp%d" % order[1]], 1)
+    g.sync.dma_start(y_block(order[1]), staged(order[1])).then_inc(S.st, 16)
+
+    g.scalar.wait_ge(S["mm%d" % nfar], 1)
+    g.scalar.activation(staged(nfar), product(nfar), ActivationFunctionType.Copy).then_inc(S["cp%d" % nfar], 1)
+    g.scalar.wait_ge(S["cp%d" % nfar], 1)
+    g.scalar.dma_start(y_block(nfar), staged(nfar)).then_inc(S.sf, 16)
+
+    g.wait_ge(S.sent, sent[0])
+    g.sync.wait_ge(S.st, 48)
+    g.scalar.wait_ge(S.sf, 16)

@@ -4,6 +4,9 @@ from concourse.mybir import dt, ActivationFunctionType
 N = 4
 SLOT = 256
 BANK = 512
+CUT = 80
+MINC = 40
+NP = 5
 
 SCRATCH = {
     "xb": ("sbuf", [128, 4 * SLOT], "bfloat16"),
@@ -16,7 +19,7 @@ SCRATCH = {
     "yb": ("sbuf", [128, N * SLOT], "float32"),
 }
 SEMAPHORES = (["xl", "wl", "qx", "qw", "sent", "st", "sf"]
-              + ["%s%d" % (p, j) for p in ("ca", "cb", "sc", "mm", "cp") for j in range(N)])
+              + ["%s_%d" % (p, j) for p in ["p%d" % i for i in range(NP)] + ["r", "s", "mm", "cp"] for j in range(N)])
 
 
 def rank_program(g, core, T, topo):
@@ -39,97 +42,110 @@ def rank_program(g, core, T, topo):
     def by_cable(j):
         return [k for k in near(j) if k != by_switch(j)][0]
 
-    def engines(a, b):
+    def mask(a, b):
         m = topo.mask(cores[a], cores[b])
-        return [1 << i for i in range(16) if (m >> i) & 1]
-
-    def own_mask(a, b):
-        e = engines(a, b)
+        e = [1 << i for i in range(16) if (m >> i) & 1]
         return e[0::2] if b == by_switch(a) else e[1::2]
 
-    def dst_id(k):
-        rid, pid = topo.addr(cores[k], core)
-        return DstId(rid=rid, pnc=pid)
+    def plan(j):
+        w, ks, kc = wid[j], by_switch(j), by_cable(j)
+        share = min(max((5 * wid[kc] + 5 * w - 5 * wid[ks]) // 2, 0), 5 * w)
+        plane_by = ks if share >= w else kc
+        ca = (share - w) // 4 if plane_by == ks else share // 4
+        ca = 0 if ca < MINC else (w if w - ca < MINC else ca)
+        names = ["p%d" % i for i in range(NP)]
 
-    def cols(j, piece):
-        h = wid[j] // 2
-        a, b = {"a": (0, h), "b": (h, wid[j]), "all": (0, wid[j])}[piece]
-        return j * SLOT + a, j * SLOT + b
+        def cut(a, b):
+            k = -(-(b - a) // CUT)
+            edges = [a + (b - a) * i // k for i in range(k + 1)] if k else []
+            return [(names.pop(0), edges[i], edges[i + 1]) for i in range(k)]
 
-    def codes(j, piece):
-        a, b = cols(j, piece)
-        return T.cx[:, a:b]
+        s = [("s", 0, w)]
+        relay = {ks: cut(0, ca) + (s if plane_by == ks else []), kc: cut(ca, w) + (s if plane_by == kc else [])}
+        rest = {ks: [("r", ca, w)] if ca < w else [], kc: [("r", 0, ca)] if ca > 0 else []}
+        sends = {k: relay[k] + rest[k] + (s if plane_by != k else []) for k in (ks, kc)}
+        return relay, sends
 
-    def plane(j, piece="all"):
-        a, b = cols(j, piece)
-        return T.sx[:, a:b]
+    plans = [plan(j) for j in range(N)]
 
-    def wire(j, what):
-        if what == "s":
-            return plane(j), S["sc%d" % j]
-        return codes(j, what).bitcast(dt.uint8), S["c%s%d" % (what, j)]
+    def width(p):
+        return (p[2] - p[1]) * (1 if p[0] == "s" else 4)
 
-    def landed(j, what):
+    def view(j, p):
+        a, b = j * SLOT + p[1], j * SLOT + p[2]
+        return T.sx[:, a:b] if p[0] == "s" else T.cx[:, a:b].bitcast(dt.uint8)
+
+    def sem(j, p):
+        return S["%s_%d" % (p[0], j)]
+
+    def needs(j):
+        relay, sends = plans[j]
         if j in near(r):
-            return len(own_mask(j, r))
-        relay = by_cable(j) if what == "b" else by_switch(j)
-        return len(engines(relay, r))
+            return [(p, len(mask(j, r))) for p in sends[r]]
+        return [(p, len(mask(k, r))) for k in near(j) for p in relay[k]]
 
-    nsw, ncb, nfar = by_switch(r), by_cable(r), far(r)
-    w_r = wid[r]
+    def codes(j):
+        return T.cx[:, j * SLOT:j * SLOT + wid[j]]
+
+    def plane(j):
+        return T.sx[:, j * SLOT:j * SLOT + wid[j]]
+
+    nfar, w_r = far(r), wid[r]
 
     g.sync.dma_start(T.xb[:, :4 * w_r], T.x[:, :4 * w_r]).then_inc(S.xl, 16)
     g.sync.dma_start(T.wb[:], T.w[:]).then_inc(S.wl, 16)
 
     g.vector.wait_ge(S.xl, 16)
-    g.vector.quantize_mx(codes(r, "all"), plane(r), T.xb[:, :4 * w_r]).then_inc(S.qx, 1)
+    g.vector.quantize_mx(codes(r), plane(r), T.xb[:, :4 * w_r]).then_inc(S.qx, 1)
     g.vector.wait_ge(S.wl, 16)
     g.vector.quantize_mx(T.cw[:], T.sw[:], T.wb[:]).then_inc(S.qw, 1)
 
     sent = [0]
 
-    def send_both(to_switch, to_cable):
+    def write(batch):
         trs = []
-        for k, what in ((nsw, to_switch), (ncb, to_cable)):
-            ap, sem = wire(r, what)
-            m = own_mask(r, k)
-            trs.append(RemoteDMATransfer(dst_ids=[dst_id(k)], dma_engine_mask=sum(m), remote_sem=sem, src=ap, dst=ap))
+        for j, p, k in batch:
+            rid, pid = topo.addr(cores[k], core)
+            m = mask(r, k)
+            trs.append(RemoteDMATransfer(dst_ids=[DstId(rid=rid, pnc=pid)], dma_engine_mask=sum(m), remote_sem=sem(j, p),
+                                         src=view(j, p), dst=view(j, p)))
             sent[0] += len(m)
         g.remote_dma_fused(trs, local_sem=S.sent)
 
     g.wait_ge(S.qx, 1)
-    send_both("a", "b")
-    send_both("s", "s")
-    send_both("b", "a")
+    mine = plans[r][1]
+    first, second = sorted(near(r), key=lambda k: -len(mine[k]))
+    for i, p in enumerate(mine[first]):
+        o = mine[second][i] if i < len(mine[second]) else None
+        if o is not None and width(o) == width(p):
+            write([(r, p, first), (r, o, second)])
+        else:
+            write([(r, p, first)])
+            if o is not None:
+                write([(r, o, second)])
 
-    def pass_on(j, what):
-        ap, sem = wire(j, what)
-        k = far(j)
-        m = engines(r, k)
-        rid, pid = topo.addr(cores[k], core)
-        g.wait_ge(sem, landed(j, what))
-        g.remote_dma(ap, ap, sem, S.sent, pid, rid, sum(m))
-        sent[0] += len(m)
+    due = []
+    for j in near(r):
+        done = 0
+        for p, n in needs(j):
+            done += width(p)
+            if p in plans[j][0][r]:
+                due.append((done, j, p, n))
+    for _d, j, p, n in sorted(due):
+        g.wait_ge(sem(j, p), n)
+        write([(j, p, far(j))])
+
+    def product(j):
+        return T.ps[:, j * BANK:j * BANK + wid[j]]
 
     order = sorted(near(r), key=lambda j: wid[j])
-    for j in order:
-        if r == by_switch(j):
-            pass_on(j, "a")
-            pass_on(j, "s")
-        else:
-            pass_on(j, "b")
-
     g.tensor.wait_ge(S.qx, 1)
     g.tensor.wait_ge(S.qw, 1)
     for j in [r] + order + [nfar]:
         if j != r:
-            for what in ("a", "b", "s"):
-                g.tensor.wait_ge(wire(j, what)[1], landed(j, what))
-        g.tensor.matmul_mx(T.ps[:, j * BANK:j * BANK + wid[j]], T.cw[:], T.sw[:], codes(j, "all"), plane(j),
-                           True, True).then_inc(S["mm%d" % j], 1)
-
-    def product(j):
-        return T.ps[:, j * BANK:j * BANK + wid[j]]
+            for p, n in needs(j):
+                g.tensor.wait_ge(sem(j, p), n)
+        g.tensor.matmul_mx(product(j), T.cw[:], T.sw[:], codes(j), plane(j), True, True).then_inc(S["mm_%d" % j], 1)
 
     def staged(j):
         return T.yb[:, j * SLOT:j * SLOT + wid[j]]
@@ -138,19 +154,19 @@ def rank_program(g, core, T, topo):
         return T.y[:, off[j]:off[j + 1]]
 
     for j in [r] + order:
-        g.vector.wait_ge(S["mm%d" % j], 1)
-        g.vector.tensor_copy(staged(j), product(j)).then_inc(S["cp%d" % j], 1)
+        g.vector.wait_ge(S["mm_%d" % j], 1)
+        g.vector.tensor_copy(staged(j), product(j)).then_inc(S["cp_%d" % j], 1)
 
-    g.sync.wait_ge(S["cp%d" % r], 1)
-    g.sync.wait_ge(S["cp%d" % order[0]], 1)
+    g.sync.wait_ge(S["cp_%d" % r], 1)
+    g.sync.wait_ge(S["cp_%d" % order[0]], 1)
     g.sync.dma_start(y_block(r), staged(r)).then_inc(S.st, 16)
     g.sync.dma_start(y_block(order[0]), staged(order[0])).then_inc(S.st, 16)
-    g.sync.wait_ge(S["cp%d" % order[1]], 1)
+    g.sync.wait_ge(S["cp_%d" % order[1]], 1)
     g.sync.dma_start(y_block(order[1]), staged(order[1])).then_inc(S.st, 16)
 
-    g.scalar.wait_ge(S["mm%d" % nfar], 1)
-    g.scalar.activation(staged(nfar), product(nfar), ActivationFunctionType.Copy).then_inc(S["cp%d" % nfar], 1)
-    g.scalar.wait_ge(S["cp%d" % nfar], 1)
+    g.scalar.wait_ge(S["mm_%d" % nfar], 1)
+    g.scalar.activation(staged(nfar), product(nfar), ActivationFunctionType.Copy).then_inc(S["cp_%d" % nfar], 1)
+    g.scalar.wait_ge(S["cp_%d" % nfar], 1)
     g.scalar.dma_start(y_block(nfar), staged(nfar)).then_inc(S.sf, 16)
 
     g.wait_ge(S.sent, sent[0])

@@ -4,9 +4,7 @@ from concourse.mybir import dt, ActivationFunctionType
 N = 4
 SLOT = 256
 BANK = 512
-CUT = 80
-MINC = 40
-NP = 5
+PIECES = ["p0", "p1", "p2", "s"]
 
 SCRATCH = {
     "xb": ("sbuf", [128, 4 * SLOT], "bfloat16"),
@@ -19,13 +17,10 @@ SCRATCH = {
     "yb": ("sbuf", [128, N * SLOT], "float32"),
 }
 SEMAPHORES = (["xl", "wl", "qx", "qw", "sent", "st", "sf"]
-              + ["%s_%d" % (p, j) for p in ["p%d" % i for i in range(NP)] + ["r", "s", "mm", "cp"] for j in range(N)])
+              + ["%s_%d" % (p, j) for p in PIECES + ["mm", "cp"] for j in range(N)])
 
 
 def rank_program(g, core, T, topo):
-    r = T.rank_of(core)
-    if r is None:
-        return
     cores, wid = T.cores, T.tables["WID"]
     off = [sum(wid[:j]) for j in range(N + 1)]
     S = T.sem
@@ -42,47 +37,91 @@ def rank_program(g, core, T, topo):
     def by_cable(j):
         return [k for k in near(j) if k != by_switch(j)][0]
 
-    def mask(a, b):
-        m = topo.mask(cores[a], cores[b])
-        e = [1 << i for i in range(16) if (m >> i) & 1]
-        return e[0::2] if b == by_switch(a) else e[1::2]
+    span = topo.CORES_PER_CHIP
 
-    def plan(j):
-        w, ks, kc = wid[j], by_switch(j), by_cable(j)
-        share = min(max((5 * wid[kc] + 5 * w - 5 * wid[ks]) // 2, 0), 5 * w)
-        plane_by = ks if share >= w else kc
-        ca = (share - w) // 4 if plane_by == ks else share // 4
-        ca = 0 if ca < MINC else (w if w - ca < MINC else ca)
-        names = ["p%d" % i for i in range(NP)]
+    def chipmates(c):
+        return [d for d in range(max(c - span, 0), c + span)
+                if d != c and topo.host(d) == topo.host(c) and topo.chip(d) == topo.chip(c)]
 
-        def cut(a, b):
-            k = -(-(b - a) // CUT)
-            edges = [a + (b - a) * i // k for i in range(k + 1)] if k else []
-            return [(names.pop(0), edges[i], edges[i + 1]) for i in range(k)]
+    def owns_port(c):
+        return all(topo.may_write(c, d) for d in range(max(c - 2 * span, 0), c + 2 * span) if topo.mates(c, d))
 
-        s = [("s", 0, w)]
-        relay = {ks: cut(0, ca) + (s if plane_by == ks else []), kc: cut(ca, w) + (s if plane_by == kc else [])}
-        rest = {ks: [("r", ca, w)] if ca < w else [], kc: [("r", 0, ca)] if ca > 0 else []}
-        sends = {k: relay[k] + rest[k] + (s if plane_by != k else []) for k in (ks, kc)}
-        return relay, sends
+    def helper(j, k):
+        c = cores[j]
+        if k == by_switch(j):
+            return [d for d in chipmates(c) if topo.die(d) != topo.die(c)][0]
+        return [d for d in chipmates(c) if topo.die(d) == topo.die(c) and owns_port(d) != owns_port(c)][0]
 
-    plans = [plan(j) for j in range(N)]
+    def bits(m):
+        return [1 << i for i in range(16) if (m >> i) & 1]
 
-    def width(p):
-        return (p[2] - p[1]) * (1 if p[0] == "s" else 4)
+    def lane(j, k):
+        e = bits(topo.mask(cores[j], cores[k]))
+        return e[0::2] if k == by_switch(j) else e[1::2]
+
+    def hand_lane(j, k):
+        e = bits(topo.mask(cores[j], helper(j, k)) & ~topo.mask(cores[j], cores[k]))
+        return e[0::2] if k == by_switch(j) else e[1::2]
+
+    def help_lane(j, k):
+        return bits(topo.mask(helper(j, k), cores[k]))[0::2]
+
+    def span_of(j, p):
+        w = wid[j]
+        ca = (3 * w + 4) // 8
+        return {"p0": (0, ca), "p1": (ca, 2 * ca), "p2": (2 * ca, w), "s": (0, w)}[p]
+
+    def straight(j, k):
+        return ["p0", "s"] if k == by_switch(j) else ["p1", "p2"]
+
+    def handed(j, k):
+        return [p for p in ["p0", "p1", "p2", "s"] if p not in straight(j, k)]
+
+    def width(j, p):
+        a, b = span_of(j, p)
+        return (b - a) * (1 if p == "s" else 4)
 
     def view(j, p):
-        a, b = j * SLOT + p[1], j * SLOT + p[2]
-        return T.sx[:, a:b] if p[0] == "s" else T.cx[:, a:b].bitcast(dt.uint8)
+        a, b = span_of(j, p)
+        a, b = j * SLOT + a, j * SLOT + b
+        return T.sx[:, a:b] if p == "s" else T.cx[:, a:b].bitcast(dt.uint8)
 
     def sem(j, p):
-        return S["%s_%d" % (p[0], j)]
+        return S["%s_%d" % (p, j)]
+
+    sent = [0]
+
+    def write(batch):
+        trs = []
+        for j, p, d, m in batch:
+            rid, pid = topo.addr(d, core)
+            trs.append(RemoteDMATransfer(dst_ids=[DstId(rid=rid, pnc=pid)], dma_engine_mask=sum(m), remote_sem=sem(j, p),
+                                         src=view(j, p), dst=view(j, p)))
+            sent[0] += len(m)
+        g.remote_dma_fused(trs, local_sem=S.sent)
+
+    def write_pair(a, b):
+        if width(a[0], a[1]) == width(b[0], b[1]):
+            write([a, b])
+        else:
+            write([a])
+            write([b])
+
+    r = T.rank_of(core)
+    if r is None:
+        for j in range(N):
+            for k in near(j):
+                if helper(j, k) == core:
+                    for p in handed(j, k):
+                        g.wait_ge(sem(j, p), len(hand_lane(j, k)))
+                        write([(j, p, cores[k], help_lane(j, k))])
+                    g.wait_ge(S.sent, sent[0])
+        return
 
     def needs(j):
-        relay, sends = plans[j]
         if j in near(r):
-            return [(p, len(mask(j, r))) for p in sends[r]]
-        return [(p, len(mask(k, r))) for k in near(j) for p in relay[k]]
+            return [(p, len(lane(j, r))) for p in straight(j, r)] + [(p, len(help_lane(j, r))) for p in handed(j, r)]
+        return [(p, len(lane(k, r))) for k in near(j) for p in straight(j, k)]
 
     def codes(j):
         return T.cx[:, j * SLOT:j * SLOT + wid[j]]
@@ -91,6 +130,7 @@ def rank_program(g, core, T, topo):
         return T.sx[:, j * SLOT:j * SLOT + wid[j]]
 
     nfar, w_r = far(r), wid[r]
+    ks, kc = by_switch(r), by_cable(r)
 
     g.sync.dma_start(T.xb[:, :4 * w_r], T.x[:, :4 * w_r]).then_inc(S.xl, 16)
     g.sync.dma_start(T.wb[:], T.w[:]).then_inc(S.wl, 16)
@@ -100,40 +140,27 @@ def rank_program(g, core, T, topo):
     g.vector.wait_ge(S.wl, 16)
     g.vector.quantize_mx(T.cw[:], T.sw[:], T.wb[:]).then_inc(S.qw, 1)
 
-    sent = [0]
+    def out(p, k):
+        return (r, p, cores[k], lane(r, k))
 
-    def write(batch):
-        trs = []
-        for j, p, k in batch:
-            rid, pid = topo.addr(cores[k], core)
-            m = mask(r, k)
-            trs.append(RemoteDMATransfer(dst_ids=[DstId(rid=rid, pnc=pid)], dma_engine_mask=sum(m), remote_sem=sem(j, p),
-                                         src=view(j, p), dst=view(j, p)))
-            sent[0] += len(m)
-        g.remote_dma_fused(trs, local_sem=S.sent)
+    def over(p, k):
+        return (r, p, helper(r, k), hand_lane(r, k))
 
     g.wait_ge(S.qx, 1)
-    mine = plans[r][1]
-    first, second = sorted(near(r), key=lambda k: -len(mine[k]))
-    for i, p in enumerate(mine[first]):
-        o = mine[second][i] if i < len(mine[second]) else None
-        if o is not None and width(o) == width(p):
-            write([(r, p, first), (r, o, second)])
-        else:
-            write([(r, p, first)])
-            if o is not None:
-                write([(r, o, second)])
+    write_pair(out("p0", ks), out("p1", kc))
+    write_pair(over("p1", ks), over("p0", kc))
+    write_pair(out("s", ks), out("p2", kc))
+    write_pair(over("p2", ks), over("s", kc))
 
     due = []
     for j in near(r):
         done = 0
-        for p, n in needs(j):
-            done += width(p)
-            if p in plans[j][0][r]:
-                due.append((done, j, p, n))
-    for _d, j, p, n in sorted(due):
-        g.wait_ge(sem(j, p), n)
-        write([(j, p, far(j))])
+        for p in straight(j, r):
+            done += width(j, p)
+            due.append((done, j, p))
+    for _d, j, p in sorted(due):
+        g.wait_ge(sem(j, p), len(lane(j, r)))
+        write([(j, p, cores[far(j)], lane(r, far(j)))])
 
     def product(j):
         return T.ps[:, j * BANK:j * BANK + wid[j]]

from concourse.bass import DstId, RemoteDMATransfer
from concourse.mybir import dt, ActivationFunctionType

N = 4
SLOT = 256
BANK = 512
PIECES = ["p0", "p1", "p2", "s"]

SCRATCH = {
    "xb": ("sbuf", [128, 4 * SLOT], "bfloat16"),
    "wb": ("sbuf", [128, 512], "bfloat16"),
    "cw": ("sbuf", [128, 128], "float8_e4m3fn_x4"),
    "sw": ("sbuf", [128, 128], "uint8"),
    "cx": ("sbuf", [128, N * SLOT], "float8_e4m3fn_x4"),
    "sx": ("sbuf", [128, N * SLOT], "uint8"),
    "ps": ("psum", [128, N * BANK], "float32"),
    "yb": ("sbuf", [128, N * SLOT], "float32"),
}
SEMAPHORES = (["xl", "wl", "qx", "qw", "sent", "st", "sf"]
              + ["%s_%d" % (p, j) for p in PIECES + ["mm", "cp"] for j in range(N)])


def rank_program(g, core, T, topo):
    cores, wid = T.cores, T.tables["WID"]
    off = [sum(wid[:j]) for j in range(N + 1)]
    S = T.sem

    def near(j):
        return [k for k in range(N) if k != j and topo.may_write(cores[j], cores[k])]

    def far(j):
        return [k for k in range(N) if k != j and k not in near(j)][0]

    def by_switch(j):
        return [k for k in near(j) if topo.same_plane(cores[j], cores[k])][0]

    def by_cable(j):
        return [k for k in near(j) if k != by_switch(j)][0]

    span = topo.CORES_PER_CHIP

    def chipmates(c):
        return [d for d in range(max(c - span, 0), c + span)
                if d != c and topo.host(d) == topo.host(c) and topo.chip(d) == topo.chip(c)]

    def owns_port(c):
        return all(topo.may_write(c, d) for d in range(max(c - 2 * span, 0), c + 2 * span) if topo.mates(c, d))

    def helper(j, k):
        c = cores[j]
        if k == by_switch(j):
            return [d for d in chipmates(c) if topo.die(d) != topo.die(c)][0]
        return [d for d in chipmates(c) if topo.die(d) == topo.die(c) and owns_port(d) != owns_port(c)][0]

    def bits(m):
        return [1 << i for i in range(16) if (m >> i) & 1]

    def lane(j, k):
        e = bits(topo.mask(cores[j], cores[k]))
        return e[0::2] if k == by_switch(j) else e[1::2]

    def hand_lane(j, k):
        e = bits(topo.mask(cores[j], helper(j, k)) & ~topo.mask(cores[j], cores[k]))
        return e[0::2] if k == by_switch(j) else e[1::2]

    def help_lane(j, k):
        return bits(topo.mask(helper(j, k), cores[k]))[0::2]

    def span_of(j, p):
        w = wid[j]
        ca = (3 * w + 4) // 8
        return {"p0": (0, ca), "p1": (ca, 2 * ca), "p2": (2 * ca, w), "s": (0, w)}[p]

    def straight(j, k):
        return ["p0", "s"] if k == by_switch(j) else ["p1", "p2"]

    def handed(j, k):
        return [p for p in ["p0", "p1", "p2", "s"] if p not in straight(j, k)]

    def width(j, p):
        a, b = span_of(j, p)
        return (b - a) * (1 if p == "s" else 4)

    def view(j, p):
        a, b = span_of(j, p)
        a, b = j * SLOT + a, j * SLOT + b
        return T.sx[:, a:b] if p == "s" else T.cx[:, a:b].bitcast(dt.uint8)

    def sem(j, p):
        return S["%s_%d" % (p, j)]

    sent = [0]

    def write(batch):
        trs = []
        for j, p, d, m in batch:
            rid, pid = topo.addr(d, core)
            trs.append(RemoteDMATransfer(dst_ids=[DstId(rid=rid, pnc=pid)], dma_engine_mask=sum(m), remote_sem=sem(j, p),
                                         src=view(j, p), dst=view(j, p)))
            sent[0] += len(m)
        g.remote_dma_fused(trs, local_sem=S.sent)

    def write_pair(a, b):
        if width(a[0], a[1]) == width(b[0], b[1]):
            write([a, b])
        else:
            write([a])
            write([b])

    r = T.rank_of(core)
    if r is None:
        for j in range(N):
            for k in near(j):
                if helper(j, k) == core:
                    for p in handed(j, k):
                        g.wait_ge(sem(j, p), len(hand_lane(j, k)))
                        write([(j, p, cores[k], help_lane(j, k))])
                    g.wait_ge(S.sent, sent[0])
        return

    def needs(j):
        if j in near(r):
            return [(p, len(lane(j, r))) for p in straight(j, r)] + [(p, len(help_lane(j, r))) for p in handed(j, r)]
        return [(p, len(lane(k, r))) for k in near(j) for p in straight(j, k)]

    def codes(j):
        return T.cx[:, j * SLOT:j * SLOT + wid[j]]

    def plane(j):
        return T.sx[:, j * SLOT:j * SLOT + wid[j]]

    nfar, w_r = far(r), wid[r]
    ks, kc = by_switch(r), by_cable(r)

    g.sync.dma_start(T.xb[:, :4 * w_r], T.x[:, :4 * w_r]).then_inc(S.xl, 16)
    g.sync.dma_start(T.wb[:], T.w[:]).then_inc(S.wl, 16)

    g.vector.wait_ge(S.xl, 16)
    g.vector.quantize_mx(codes(r), plane(r), T.xb[:, :4 * w_r]).then_inc(S.qx, 1)
    g.vector.wait_ge(S.wl, 16)
    g.vector.quantize_mx(T.cw[:], T.sw[:], T.wb[:]).then_inc(S.qw, 1)

    def out(p, k):
        return (r, p, cores[k], lane(r, k))

    def over(p, k):
        return (r, p, helper(r, k), hand_lane(r, k))

    g.wait_ge(S.qx, 1)
    write_pair(out("p0", ks), out("p1", kc))
    write_pair(over("p1", ks), over("p0", kc))
    write_pair(out("s", ks), out("p2", kc))
    write_pair(over("p2", ks), over("s", kc))

    due = []
    for j in near(r):
        done = 0
        for p in straight(j, r):
            done += width(j, p)
            due.append((done, j, p))
    for _d, j, p in sorted(due):
        g.wait_ge(sem(j, p), len(lane(j, r)))
        write([(j, p, cores[far(j)], lane(r, far(j)))])

    def product(j):
        return T.ps[:, j * BANK:j * BANK + wid[j]]

    order = sorted(near(r), key=lambda j: wid[j])
    g.tensor.wait_ge(S.qx, 1)
    g.tensor.wait_ge(S.qw, 1)
    for j in [r] + order + [nfar]:
        if j != r:
            for p, n in needs(j):
                g.tensor.wait_ge(sem(j, p), n)
        g.tensor.matmul_mx(product(j), T.cw[:], T.sw[:], codes(j), plane(j), True, True).then_inc(S["mm_%d" % j], 1)

    def staged(j):
        return T.yb[:, j * SLOT:j * SLOT + wid[j]]

    def y_block(j):
        return T.y[:, off[j]:off[j + 1]]

    for j in [r] + order:
        g.vector.wait_ge(S["mm_%d" % j], 1)
        g.vector.tensor_copy(staged(j), product(j)).then_inc(S["cp_%d" % j], 1)

    g.sync.wait_ge(S["cp_%d" % r], 1)
    g.sync.wait_ge(S["cp_%d" % order[0]], 1)
    g.sync.dma_start(y_block(r), staged(r)).then_inc(S.st, 16)
    g.sync.dma_start(y_block(order[0]), staged(order[0])).then_inc(S.st, 16)
    g.sync.wait_ge(S["cp_%d" % order[1]], 1)
    g.sync.dma_start(y_block(order[1]), staged(order[1])).then_inc(S.st, 16)

    g.scalar.wait_ge(S["mm_%d" % nfar], 1)
    g.scalar.activation(staged(nfar), product(nfar), ActivationFunctionType.Copy).then_inc(S["cp_%d" % nfar], 1)
    g.scalar.wait_ge(S["cp_%d" % nfar], 1)
    g.scalar.dma_start(y_block(nfar), staged(nfar)).then_inc(S.sf, 16)

    g.wait_ge(S.sent, sent[0])
    g.sync.wait_ge(S.st, 48)
    g.scalar.wait_ge(S.sf, 16)
